import numpy as np
import ml_dtypes


def mxq(x, axis, fmt="e4m3"):
    dtype, down = {"e4m3": (ml_dtypes.float8_e4m3fn, 7), "e5m2": (ml_dtypes.float8_e5m2, 14)}[fmt]
    v = np.moveaxis(np.asarray(x, np.float32).astype(ml_dtypes.bfloat16).astype(np.float64), axis, -1)
    blocks = v.reshape(v.shape[:-1] + (-1, 32))
    amax = np.abs(blocks).max(-1, keepdims=True)
    byte = np.maximum(np.where(amax > 0, np.frexp(amax)[1] - 1 + 127, 0) - down, 1)
    scale = np.exp2(byte - 127.0)
    codes = (blocks / scale).astype(np.float32).astype(dtype).astype(np.float64)
    return np.moveaxis((codes * scale).reshape(v.shape), -1, axis)


WIDE = False


def mx_kscale(k):
    if not WIDE:
        return np.ones(k)
    levels = np.array([10, -10, 5, -5, 0])
    if k % 512:
        return np.exp2(np.random.permutation(np.resize(levels, k // 32))).repeat(32)
    a = np.empty((k // 512, 16))
    for p in range(k // 512):
        a[p, :8] = np.random.permutation(np.resize(levels, 8))
        for g in range(8):
            far = levels[np.abs(levels - a[p, g]) >= 10]
            a[p, g + 8] = far[np.random.randint(len(far))]
    return np.exp2(a.ravel()).repeat(32)


def f64(x):
    return np.asarray(x).astype(np.float64)


def striped(idx):
    return np.tile(idx.reshape(-1, 16).T, (8, 1)).astype(np.uint16)


def unstriped(offs):
    return offs[:16].T.reshape(-1).astype(np.int64)


def striped8(idx):
    return np.concatenate([x.reshape(-1, 16).T for x in idx]).astype(np.uint16)


def runs(offs, k):
    lists = np.stack([offs[16 * r : 16 * r + 16].T.reshape(-1) for r in range(8)]).astype(np.int64)
    return lists[np.arange(k) % 512 // 64]


def pack_weight(w):
    k, n = w.shape
    w = f64(np.asarray(w, np.float32).astype(ml_dtypes.bfloat16)).reshape(k // 32, 32, n)
    amax = np.abs(w).max(1)
    byte = np.clip(np.where(amax > 0, np.frexp(amax)[1] - 1 + 127 - 7, 1), 1, 254)
    scaled = (w * np.exp2(127.0 - byte)[:, None, :]).reshape(k, n).astype(np.float32)
    words = np.ascontiguousarray(scaled.reshape(k // 512, 128, 4, n).transpose(0, 1, 3, 2)).astype(ml_dtypes.float8_e4m3fn).view(np.uint8)
    return words, np.ascontiguousarray(byte.astype(np.uint8).reshape(k // 512, 16, n))


def unpack_weight(words, scales):
    g, p, n, _ = words.shape
    vals = np.ascontiguousarray(words).view(ml_dtypes.float8_e4m3fn).astype(np.float64) * np.repeat(np.exp2(scales.astype(np.float64) - 127.0), 8, axis=1)[..., None]
    return vals.transpose(0, 1, 3, 2).reshape(g * 512, n)


K, T, S, H, W, G = 512, 1024, 256, 512, 128, 2048


def setup_inputs():
    n = np.random.standard_normal
    s = mx_kscale(K)[:, None]
    packed_xT = pack_weight(n((K, T)) * s)
    packed_dT = pack_weight(n((K, G)) / s)
    perm = np.random.permutation(S)
    return {
        "x_words": packed_xT[0],
        "x_scales": packed_xT[1],
        "w1": (n((K, H)) / np.sqrt(K) / s).astype(np.float32),
        "gs": (np.random.uniform(0.5, 1.5, (K, 1)) * s).astype(np.float32),
        "d_words": packed_dT[0],
        "d_scales": packed_dT[1],
        "offs": striped(np.random.permutation(T)[:S]),
        "n1": striped(perm[:W]),
        "n2": striped(perm[W:]),
        "k1": striped8(np.random.randint(0, G, (8, H))),
        "k2": striped8(np.random.randint(0, G, (8, H))),
        "two": striped(np.random.permutation(T)[:S]),
        "n3": striped(np.random.permutation(S)),
        "n4": striped(np.random.permutation(S)),
    }


def reference(x_words, x_scales, w1, gs, d_words, d_scales, offs, n1, n2, k1, k2, two, n3, n4):
    d_k1 = unpack_weight(d_words, d_scales)[np.arange(K)[:, None], runs(k1, K)]
    xq = unpack_weight(x_words, x_scales)[:, unstriped(offs)]
    y = mxq(f64(w1), 0, "e4m3").T @ xq
    pa = y[:, unstriped(n1)]
    pb = y[:, unstriped(n2)]
    rb = pa - pb
    ra = 0.75 * (pa + pb)
    ds = np.zeros((H, S))
    ds[:, unstriped(n1)] = ra
    dt = ds.copy()
    dt[:, unstriped(n2)] = rb
    z = f64(gs) * dt
    d_k2 = unpack_weight(d_words, d_scales)[np.arange(K)[:, None], runs(k2, K)]
    x_two = unpack_weight(x_words, x_scales)[:, unstriped(two)]
    h = 0.0625 * ((d_k1.T @ mxq(z, 0, "e4m3") + d_k2.T @ x_two))
    st = np.maximum(h, h[:, unstriped(n3)])
    ds2 = np.zeros((H, S))
    ds2[:, unstriped(n4)] = st
    return ds2 - h

@@ -1,0 +1,165 @@
+from contextlib import ExitStack
+
+import concourse.mybir as mybir
+
+K, T, S, H, W, G = 512, 1024, 256, 512, 128, 2048
+FLOPS = 3 * 2 * K * H * S
+
+F32 = mybir.dt.float32
+BF16 = mybir.dt.bfloat16
+I32 = mybir.dt.int32
+U32 = mybir.dt.uint32
+U16 = mybir.dt.uint16
+U8 = mybir.dt.uint8
+FP8X4 = mybir.dt.float8_e4m3fn_x4
+ALU = mybir.AluOpType
+COPY = mybir.ActivationFunctionType.Copy
+
+P = 128
+PACK = 4
+TILES = H // P
+GATHER_WINDOW = 272
+SCATTER_WINDOW = 352
+
+
+def tile_picked_cmixhaarsendhop_none_p_kernel(
+    tc, x_words, x_scales, w1, gs, d_words, d_scales, offs, n1, n2, k1, k2, two, n3, n4, out
+):
+    nc = tc.nc
+    with ExitStack() as ctx:
+        keep = ctx.enter_context(tc.tile_pool(name="keep", bufs=1))
+        psum = ctx.enter_context(tc.psum_pool(name="psum", bufs=1))
+
+        def load_list(name, src):
+            entries = keep.tile(list(src.shape), U16, name=name)
+            nc.sync.dma_start(entries[:], src)
+            return entries
+
+        x_byte_table = keep.tile([P, T], U8, align_bytes=64)
+        nc.vector.memset(x_byte_table[:].bitcast(I32), 0)
+        offs_sb = load_list("offs_sb", offs)
+        for r in range(4):
+            nc.sync.dma_start(x_byte_table[r:P:32, :].bitcast(I32), x_scales[0][r:16:4, :].bitcast(I32))
+
+        w_rows = w1.rearrange("(p j) c -> p j c", j=PACK)
+        w_raw = []
+        for half in range(2):
+            raw = keep.tile([P, PACK, H // 2], F32, name=f"w_raw{half}")
+            nc.sync.dma_start(raw[:], w_rows[:, :, half * (H // 2) : (half + 1) * (H // 2)])
+            w_raw.append(raw)
+        x_word_table = keep.tile([P, T], I32, align_bytes=64)
+        nc.sync.dma_start(x_word_table[:], x_words[0].rearrange("p n r -> p (n r)").bitcast(I32))
+
+        n1_sb = load_list("n1_sb", n1)
+        n2_sb = load_list("n2_sb", n2)
+        two_sb = load_list("two_sb", two)
+        k1_sb = load_list("k1_sb", k1)
+        k2_sb = load_list("k2_sb", k2)
+        d_byte_table = keep.tile([P, G], U8, align_bytes=64)
+        nc.gpsimd.memset(d_byte_table[:].bitcast(I32), 0)
+        nc.sync.dma_start(d_byte_table[0:P:8, :].bitcast(I32), d_scales[0].bitcast(I32))
+        d_word_table = keep.tile([P, G], I32, align_bytes=64)
+        nc.sync.dma_start(d_word_table[:], d_words[0].rearrange("p n r -> p (n r)").bitcast(I32))
+        gs_sb = keep.tile([P, PACK], F32)
+        nc.sync.dma_start(gs_sb[:], gs.rearrange("(p t) o -> p (t o)", t=PACK))
+        n3_sb = load_list("n3_sb", n3)
+        n4_sb = load_list("n4_sb", n4)
+
+        xq_bytes = keep.tile([P, S], U8, align_bytes=64)
+        nc.vector.tensor_copy(xq_bytes[:], x_byte_table[:].indirect(offs_sb[:]))
+
+        w_bf = keep.tile([P, TILES, P, PACK], BF16, align_bytes=64)
+        for half, copy in enumerate((nc.scalar.copy, nc.vector.tensor_copy)):
+            copy(
+                w_bf[:, :, half * 64 : (half + 1) * 64, :].rearrange("p t m j -> p m j t"),
+                w_raw[half][:].rearrange("p j (m t) -> p m j t", t=TILES),
+            )
+        w_codes = [keep.tile([P, P], U32, name=f"w_codes{t}", align_bytes=64) for t in range(TILES)]
+        w_bytes = [keep.tile([P, P], U8, name=f"w_bytes{t}", align_bytes=64) for t in range(TILES)]
+
+        def quantise_w(t):
+            nc.vector.quantize_mx(w_codes[t][:].bitcast(FP8X4), w_bytes[t][:], w_bf[:, t].rearrange("p m j -> p (m j)"))
+
+        quantise_w(0)
+        xq_words = keep.tile([P, S], U32, align_bytes=64)
+        nc.vector.tensor_copy(xq_words[:], x_word_table[:].bitcast(U32).indirect(offs_sb[:]))
+        for t in range(1, TILES):
+            quantise_w(t)
+
+        y_sb, pa, pb = [], [], []
+        for t in range(TILES):
+            acc = psum.tile([P, S], F32, name=f"y_acc{t}")
+            nc.tensor.matmul_mx(acc[:], w_codes[t][:].bitcast(FP8X4), w_bytes[t][:], xq_words[:].bitcast(FP8X4), xq_bytes[:], start=True, stop=True)
+            y = keep.tile([P, S], F32, name=f"y{t}")
+            (nc.scalar.copy if t == 0 else nc.vector.tensor_copy)(y[:], acc[:])
+            y_sb.append(y)
+        ra, rb = [], []
+        for t in range(TILES):
+            a = keep.tile([P, W], F32, name=f"pa{t}")
+            b = keep.tile([P, W], F32, name=f"pb{t}")
+            nc.scalar.activation(a[:], y_sb[t][:].indirect(n1_sb[:]), COPY)
+            nc.scalar.activation(b[:], y_sb[t][:].indirect(n2_sb[:]), COPY)
+            s = keep.tile([P, W], F32, name=f"sum{t}")
+            d = keep.tile([P, W], F32, name=f"rb{t}")
+            nc.vector.tensor_tensor(s[:], a[:], b[:], ALU.add)
+            nc.vector.tensor_tensor(d[:], a[:], b[:], ALU.subtract)
+            ra.append(s)
+            rb.append(d)
+
+        x2_bytes = keep.tile([P, S], U8, align_bytes=64)
+        x2_words = keep.tile([P, S], U32, align_bytes=64)
+        d_picked_bytes = keep.tile([P, 2 * H], U8, align_bytes=64)
+        d_bytes = keep.tile([P, 2 * H], U8, align_bytes=64)
+        nc.gpsimd.memset(d_bytes[:].bitcast(I32), 0)
+        nc.vector.tensor_copy(d_picked_bytes[:, 0:H], d_byte_table[:].indirect(k1_sb[:]))
+        nc.vector.tensor_copy(d_picked_bytes[:, H : 2 * H], d_byte_table[:].indirect(k2_sb[:]))
+        for r in range(4):
+            nc.sync.dma_start(d_bytes[r:P:32, :].bitcast(I32), d_picked_bytes[8 * r : P : 32, :].bitcast(I32))
+        nc.vector.tensor_copy(x2_bytes[:], x_byte_table[:].indirect(two_sb[:]))
+        nc.vector.tensor_copy(x2_words[:], x_word_table[:].bitcast(U32).indirect(two_sb[:]))
+        d1_words = [keep.tile([P, H // 2], U32, name=f"d1_words{u}", align_bytes=64) for u in range(2)]
+        d2_words = [keep.tile([P, H // 2], U32, name=f"d2_words{u}", align_bytes=64) for u in range(2)]
+
+        def gather_d_words(u):
+            for words, lst in ((d2_words, k2_sb), (d1_words, k1_sb)):
+                nc.vector.tensor_copy(words[u][:], d_word_table[:].bitcast(U32).indirect(lst[:, 16 * u : 16 * (u + 1)]))
+
+        z_bf = keep.tile([P, S, PACK], BF16, align_bytes=64)
+        for t in range(TILES):
+            dt = keep.tile([P, S], F32, name=f"dt{t}")
+            nc.scalar.activation(dt[:].indirect(n1_sb[:]), ra[t][:], COPY, scale=0.75)
+            nc.scalar.activation(dt[:].indirect(n2_sb[:]), rb[t][:], COPY)
+            nc.vector.tensor_scalar(z_bf[:, :, t], dt[:], gs_sb[:, t : t + 1], None, ALU.mult)
+            if t < 2:
+                gather_d_words(t)
+
+        h_acc = [psum.tile([P, S], F32, name=f"h_acc{t}") for t in range(TILES)]
+        for t in range(TILES):
+            cols = slice((t % 2) * P, (t % 2 + 1) * P)
+            nc.tensor.matmul_mx(h_acc[t][:], d2_words[t // 2][:, cols].bitcast(FP8X4), d_bytes[:, H + t * P : H + (t + 1) * P], x2_words[:].bitcast(FP8X4), x2_bytes[:], start=True, stop=False)
+        z_codes = keep.tile([P, S], U32, align_bytes=64)
+        z_bytes = keep.tile([P, S], U8, align_bytes=64)
+        nc.vector.quantize_mx(z_codes[:].bitcast(FP8X4), z_bytes[:], z_bf[:].rearrange("p s j -> p (s j)"))
+        h_sb = []
+        for t in range(TILES):
+            cols = slice((t % 2) * P, (t % 2 + 1) * P)
+            nc.tensor.matmul_mx(h_acc[t][:], d1_words[t // 2][:, cols].bitcast(FP8X4), d_bytes[:, t * P : (t + 1) * P], z_codes[:].bitcast(FP8X4), z_bytes[:], start=False, stop=True)
+            h = keep.tile([P, GATHER_WINDOW], F32, name=f"h{t}")
+            if t == 0:
+                nc.scalar.activation(h[:, 0:S], h_acc[t][:], COPY, scale=0.0625)
+            else:
+                nc.vector.tensor_scalar(h[:, 0:S], h_acc[t][:], 0.0625, None, ALU.mult)
+            h_sb.append(h)
+        st_sb = []
+        for t in range(TILES):
+            hop = keep.tile([P, S], F32, name=f"hop{t}")
+            nc.scalar.activation(hop[:], h_sb[t][:].indirect(n3_sb[:]), COPY)
+            st = keep.tile([P, S], F32, name=f"st{t}")
+            nc.vector.tensor_tensor(st[:], h_sb[t][:, 0:S], hop[:], ALU.max)
+            st_sb.append(st)
+        for t in range(TILES):
+            ds2 = keep.tile([P, SCATTER_WINDOW], F32, name=f"ds2_{t}")
+            nc.scalar.activation(ds2[:].indirect(n4_sb[:]), st_sb[t][:], COPY)
+            res = keep.tile([P, S], F32, name=f"res{t}")
+            nc.vector.tensor_tensor(res[:], ds2[:, 0:S], h_sb[t][:, 0:S], ALU.subtract)
+            nc.sync.dma_start(out[t * P : (t + 1) * P, :], res[:])

@@ -20,6 +20,8 @@ PACK = 4
 TILES = H // P
 GATHER_WINDOW = 272
 SCATTER_WINDOW = 352
+CAST_SPLIT = 40
+HALF = S // 2
 
 
 def tile_picked_cmixhaarsendhop_none_p_kernel(
@@ -37,27 +39,24 @@ def tile_picked_cmixhaarsendhop_none_p_kernel(
 
         x_byte_table = keep.tile([P, T], U8, align_bytes=64)
         nc.vector.memset(x_byte_table[:].bitcast(I32), 0)
-        offs_sb = load_list("offs_sb", offs)
-        for r in range(4):
-            nc.sync.dma_start(x_byte_table[r:P:32, :].bitcast(I32), x_scales[0][r:16:4, :].bitcast(I32))
-
         w_rows = w1.rearrange("(p j) c -> p j c", j=PACK)
-        w_raw = []
-        for half in range(2):
-            raw = keep.tile([P, PACK, H // 2], F32, name=f"w_raw{half}")
-            nc.sync.dma_start(raw[:], w_rows[:, :, half * (H // 2) : (half + 1) * (H // 2)])
-            w_raw.append(raw)
+        w_raw = [keep.tile([P, PACK, H // 2], F32, name=f"w_raw{u}") for u in range(2)]
+        nc.sync.dma_start(w_raw[0][:], w_rows[:, :, 0 : H // 2])
+        offs_sb = load_list("offs_sb", offs)
+        for q in range(4):
+            nc.sync.dma_start(x_byte_table[32 * q : 32 * q + 4, :].bitcast(I32), x_scales[0][4 * q : 4 * q + 4, :].bitcast(I32))
+        nc.sync.dma_start(w_raw[1][:], w_rows[:, :, H // 2 : H])
         x_word_table = keep.tile([P, T], I32, align_bytes=64)
         nc.sync.dma_start(x_word_table[:], x_words[0].rearrange("p n r -> p (n r)").bitcast(I32))
 
         n1_sb = load_list("n1_sb", n1)
         n2_sb = load_list("n2_sb", n2)
-        two_sb = load_list("two_sb", two)
         k1_sb = load_list("k1_sb", k1)
         k2_sb = load_list("k2_sb", k2)
         d_byte_table = keep.tile([P, G], U8, align_bytes=64)
         nc.gpsimd.memset(d_byte_table[:].bitcast(I32), 0)
         nc.sync.dma_start(d_byte_table[0:P:8, :].bitcast(I32), d_scales[0].bitcast(I32))
+        two_sb = load_list("two_sb", two)
         d_word_table = keep.tile([P, G], I32, align_bytes=64)
         nc.sync.dma_start(d_word_table[:], d_words[0].rearrange("p n r -> p (n r)").bitcast(I32))
         gs_sb = keep.tile([P, PACK], F32)
@@ -69,34 +68,32 @@ def tile_picked_cmixhaarsendhop_none_p_kernel(
         nc.vector.tensor_copy(xq_bytes[:], x_byte_table[:].indirect(offs_sb[:]))
 
         w_bf = keep.tile([P, TILES, P, PACK], BF16, align_bytes=64)
-        for half, copy in enumerate((nc.scalar.copy, nc.vector.tensor_copy)):
-            copy(
-                w_bf[:, :, half * 64 : (half + 1) * 64, :].rearrange("p t m j -> p m j t"),
-                w_raw[half][:].rearrange("p j (m t) -> p m j t", t=TILES),
-            )
-        w_codes = [keep.tile([P, P], U32, name=f"w_codes{t}", align_bytes=64) for t in range(TILES)]
-        w_bytes = [keep.tile([P, P], U8, name=f"w_bytes{t}", align_bytes=64) for t in range(TILES)]
-
-        def quantise_w(t):
-            nc.vector.quantize_mx(w_codes[t][:].bitcast(FP8X4), w_bytes[t][:], w_bf[:, t].rearrange("p m j -> p (m j)"))
-
-        quantise_w(0)
+        w_cols = [raw[:].rearrange("p j (m t) -> p m j t", t=TILES) for raw in w_raw]
+        w_dealt = w_bf[:].rearrange("p t m j -> p m j t")
+        nc.scalar.copy(w_dealt[:, 0:64], w_cols[0])
+        nc.vector.tensor_copy(w_dealt[:, 64 : 64 + CAST_SPLIT], w_cols[1][:, 0:CAST_SPLIT])
+        nc.scalar.copy(w_dealt[:, 64 + CAST_SPLIT : P], w_cols[1][:, CAST_SPLIT:64])
+        halves = [slice(u * HALF, (u + 1) * HALF) for u in range(2)]
+        whole = slice(0, S)
         xq_words = keep.tile([P, S], U32, align_bytes=64)
-        nc.vector.tensor_copy(xq_words[:], x_word_table[:].bitcast(U32).indirect(offs_sb[:]))
-        for t in range(1, TILES):
-            quantise_w(t)
+        for u in range(2):
+            nc.vector.tensor_copy(xq_words[:, halves[u]], x_word_table[:].bitcast(U32).indirect(offs_sb[:, 8 * u : 8 * (u + 1)]))
 
-        y_sb, pa, pb = [], [], []
+        y_sb = []
         for t in range(TILES):
-            acc = psum.tile([P, S], F32, name=f"y_acc{t}")
-            nc.tensor.matmul_mx(acc[:], w_codes[t][:].bitcast(FP8X4), w_bytes[t][:], xq_words[:].bitcast(FP8X4), xq_bytes[:], start=True, stop=True)
+            w_codes = keep.tile([P, P], U32, name=f"w_codes{t}", align_bytes=64)
+            w_bytes = keep.tile([P, P], U8, name=f"w_bytes{t}", align_bytes=64)
+            nc.vector.quantize_mx(w_codes[:].bitcast(FP8X4), w_bytes[:], w_bf[:, t].rearrange("p m j -> p (m j)"))
             y = keep.tile([P, S], F32, name=f"y{t}")
-            (nc.scalar.copy if t == 0 else nc.vector.tensor_copy)(y[:], acc[:])
+            for u, cols in enumerate(halves if t == 0 else [whole]):
+                acc = psum.tile([P, cols.stop - cols.start], F32, name=f"y_acc{t}_{u}")
+                nc.tensor.matmul_mx(acc[:], w_codes[:].bitcast(FP8X4), w_bytes[:], xq_words[:, cols].bitcast(FP8X4), xq_bytes[:, cols], start=True, stop=True)
+                (nc.scalar.copy if t == 0 else nc.vector.tensor_copy)(y[:, cols], acc[:])
             y_sb.append(y)
         ra, rb = [], []
         for t in range(TILES):
-            a = keep.tile([P, W], F32, name=f"pa{t}")
-            b = keep.tile([P, W], F32, name=f"pb{t}")
+            a = keep.tile([P, W], F32, name=f"pa{t}", tag=f"slot_a{t}", align_bytes=64)
+            b = keep.tile([P, W], F32, name=f"pb{t}", tag=f"slot_b{t}", align_bytes=64)
             nc.scalar.activation(a[:], y_sb[t][:].indirect(n1_sb[:]), COPY)
             nc.scalar.activation(b[:], y_sb[t][:].indirect(n2_sb[:]), COPY)
             s = keep.tile([P, W], F32, name=f"sum{t}")
@@ -106,50 +103,68 @@ def tile_picked_cmixhaarsendhop_none_p_kernel(
             ra.append(s)
             rb.append(d)
 
-        x2_bytes = keep.tile([P, S], U8, align_bytes=64)
-        x2_words = keep.tile([P, S], U32, align_bytes=64)
-        d_picked_bytes = keep.tile([P, 2 * H], U8, align_bytes=64)
+        d_picked_bytes = keep.tile([P, 2 * H], U8, tag="slot_a1", align_bytes=64)
         d_bytes = keep.tile([P, 2 * H], U8, align_bytes=64)
-        nc.gpsimd.memset(d_bytes[:].bitcast(I32), 0)
         nc.vector.tensor_copy(d_picked_bytes[:, 0:H], d_byte_table[:].indirect(k1_sb[:]))
         nc.vector.tensor_copy(d_picked_bytes[:, H : 2 * H], d_byte_table[:].indirect(k2_sb[:]))
         for r in range(4):
             nc.sync.dma_start(d_bytes[r:P:32, :].bitcast(I32), d_picked_bytes[8 * r : P : 32, :].bitcast(I32))
+        x2_bytes = keep.tile([P, S], U8, tag="slot_a2", align_bytes=64)
+        x2_words = keep.tile([P, S], U32, tag="slot_b2", align_bytes=64)
         nc.vector.tensor_copy(x2_bytes[:], x_byte_table[:].indirect(two_sb[:]))
         nc.vector.tensor_copy(x2_words[:], x_word_table[:].bitcast(U32).indirect(two_sb[:]))
-        d1_words = [keep.tile([P, H // 2], U32, name=f"d1_words{u}", align_bytes=64) for u in range(2)]
-        d2_words = [keep.tile([P, H // 2], U32, name=f"d2_words{u}", align_bytes=64) for u in range(2)]
 
-        def gather_d_words(u):
-            for words, lst in ((d2_words, k2_sb), (d1_words, k1_sb)):
-                nc.vector.tensor_copy(words[u][:], d_word_table[:].bitcast(U32).indirect(lst[:, 16 * u : 16 * (u + 1)]))
+        def gather_d_words(u, tag):
+            words = keep.tile([P, H], U32, name=f"d_picked_words{u}", tag=tag, align_bytes=64)
+            nc.vector.tensor_copy(words[:, H // 2 : H], d_word_table[:].bitcast(U32).indirect(k2_sb[:, 16 * u : 16 * (u + 1)]))
+            nc.vector.tensor_copy(words[:, 0 : H // 2], d_word_table[:].bitcast(U32).indirect(k1_sb[:, 16 * u : 16 * (u + 1)]))
+            return words
 
-        z_bf = keep.tile([P, S, PACK], BF16, align_bytes=64)
-        for t in range(TILES):
-            dt = keep.tile([P, S], F32, name=f"dt{t}")
-            nc.scalar.activation(dt[:].indirect(n1_sb[:]), ra[t][:], COPY, scale=0.75)
-            nc.scalar.activation(dt[:].indirect(n2_sb[:]), rb[t][:], COPY)
-            nc.vector.tensor_scalar(z_bf[:, :, t], dt[:], gs_sb[:, t : t + 1], None, ALU.mult)
-            if t < 2:
-                gather_d_words(t)
+        h_first = [psum.tile([P, HALF], F32, name=f"h_first{u}") for u in range(2)]
+        h_acc = {t: psum.tile([P, S], F32, name=f"h_acc{t}", tag=tag) for t, tag in ((1, "h_acc1"), (2, "y_acc0_0"), (3, "y_acc0_1"))}
 
-        h_acc = [psum.tile([P, S], F32, name=f"h_acc{t}") for t in range(TILES)]
-        for t in range(TILES):
-            cols = slice((t % 2) * P, (t % 2 + 1) * P)
-            nc.tensor.matmul_mx(h_acc[t][:], d2_words[t // 2][:, cols].bitcast(FP8X4), d_bytes[:, H + t * P : H + (t + 1) * P], x2_words[:].bitcast(FP8X4), x2_bytes[:], start=True, stop=False)
+        def add_pass(acc, words, word_col, byte_col, codes, scales, cols, first):
+            nc.tensor.matmul_mx(
+                acc[:],
+                words[:, word_col : word_col + P].bitcast(FP8X4),
+                d_bytes[:, byte_col : byte_col + P],
+                codes[:, cols].bitcast(FP8X4),
+                scales[:, cols],
+                start=first,
+                stop=not first,
+            )
+
+        early_words = gather_d_words(0, "slot_a3")
+        for u in range(2):
+            add_pass(h_first[u], early_words, H // 2, H, x2_words, x2_bytes, halves[u], True)
+        add_pass(h_acc[1], early_words, H // 2 + P, H + P, x2_words, x2_bytes, whole, True)
+
+        z_bf = keep.tile([P, S, PACK], BF16, tag="slot_z", align_bytes=64)
+        dt = [keep.tile([P, S], F32, name=f"dt{t}") for t in range(TILES)]
+        for pair in ((0, 1), (2, 3)):
+            for t in pair:
+                nc.scalar.activation(dt[t][:].indirect(n1_sb[:]), ra[t][:], COPY, scale=0.75)
+            for t in pair:
+                nc.scalar.activation(dt[t][:].indirect(n2_sb[:]), rb[t][:], COPY)
+                for cols in halves if t == TILES - 1 else [whole]:
+                    nc.vector.tensor_scalar(z_bf[:, cols, t], dt[t][:, cols], gs_sb[:, t : t + 1], None, ALU.mult)
+
         z_codes = keep.tile([P, S], U32, align_bytes=64)
         z_bytes = keep.tile([P, S], U8, align_bytes=64)
-        nc.vector.quantize_mx(z_codes[:].bitcast(FP8X4), z_bytes[:], z_bf[:].rearrange("p s j -> p (s j)"))
-        h_sb = []
-        for t in range(TILES):
-            cols = slice((t % 2) * P, (t % 2 + 1) * P)
-            nc.tensor.matmul_mx(h_acc[t][:], d1_words[t // 2][:, cols].bitcast(FP8X4), d_bytes[:, t * P : (t + 1) * P], z_codes[:].bitcast(FP8X4), z_bytes[:], start=False, stop=True)
-            h = keep.tile([P, GATHER_WINDOW], F32, name=f"h{t}")
-            if t == 0:
-                nc.scalar.activation(h[:, 0:S], h_acc[t][:], COPY, scale=0.0625)
-            else:
-                nc.vector.tensor_scalar(h[:, 0:S], h_acc[t][:], 0.0625, None, ALU.mult)
-            h_sb.append(h)
+        h_sb = [keep.tile([P, GATHER_WINDOW], F32, name=f"h{t}") for t in range(TILES)]
+        for u in range(2):
+            nc.vector.quantize_mx(z_codes[:, halves[u]].bitcast(FP8X4), z_bytes[:, halves[u]], z_bf[:, halves[u], :].rearrange("p s j -> p (s j)"))
+        for u in range(2):
+            add_pass(h_first[u], early_words, 0, 0, z_codes, z_bytes, halves[u], False)
+            nc.scalar.activation(h_sb[0][:, halves[u]], h_first[u][:], COPY, scale=0.0625)
+        add_pass(h_acc[1], early_words, P, P, z_codes, z_bytes, whole, False)
+        nc.vector.tensor_scalar(h_sb[1][:, 0:S], h_acc[1][:], 0.0625, None, ALU.mult)
+        late_words = gather_d_words(1, "slot_z")
+        for t in range(2, TILES):
+            c = (t % 2) * P
+            add_pass(h_acc[t], late_words, H // 2 + c, H + t * P, x2_words, x2_bytes, whole, True)
+            add_pass(h_acc[t], late_words, c, t * P, z_codes, z_bytes, whole, False)
+            nc.vector.tensor_scalar(h_sb[t][:, 0:S], h_acc[t][:], 0.0625, None, ALU.mult)
         st_sb = []
         for t in range(TILES):
             hop = keep.tile([P, S], F32, name=f"hop{t}")

@@ -30,6 +30,7 @@ def tile_picked_cmixhaarsendhop_none_p_kernel(
     nc = tc.nc
     with ExitStack() as ctx:
         keep = ctx.enter_context(tc.tile_pool(name="keep", bufs=1))
+        ring = ctx.enter_context(tc.tile_pool(name="ring", bufs=2))
         psum = ctx.enter_context(tc.psum_pool(name="psum", bufs=1))
 
         def load_list(name, src):
@@ -70,9 +71,9 @@ def tile_picked_cmixhaarsendhop_none_p_kernel(
         w_bf = keep.tile([P, TILES, P, PACK], BF16, align_bytes=64)
         w_cols = [raw[:].rearrange("p j (m t) -> p m j t", t=TILES) for raw in w_raw]
         w_dealt = w_bf[:].rearrange("p t m j -> p m j t")
-        nc.scalar.copy(w_dealt[:, 0:64], w_cols[0])
-        nc.vector.tensor_copy(w_dealt[:, 64 : 64 + CAST_SPLIT], w_cols[1][:, 0:CAST_SPLIT])
-        nc.scalar.copy(w_dealt[:, 64 + CAST_SPLIT : P], w_cols[1][:, CAST_SPLIT:64])
+        for u in range(2):
+            nc.vector.tensor_copy(w_dealt[:, 64 * u : 64 * u + CAST_SPLIT], w_cols[u][:, 0:CAST_SPLIT])
+            nc.scalar.copy(w_dealt[:, 64 * u + CAST_SPLIT : 64 * (u + 1)], w_cols[u][:, CAST_SPLIT:64])
         halves = [slice(u * HALF, (u + 1) * HALF) for u in range(2)]
         whole = slice(0, S)
         xq_words = keep.tile([P, S], U32, align_bytes=64)
@@ -81,8 +82,8 @@ def tile_picked_cmixhaarsendhop_none_p_kernel(
 
         y_sb = []
         for t in range(TILES):
-            w_codes = keep.tile([P, P], U32, name=f"w_codes{t}", align_bytes=64)
-            w_bytes = keep.tile([P, P], U8, name=f"w_bytes{t}", align_bytes=64)
+            w_codes = ring.tile([P, P], U32, align_bytes=64)
+            w_bytes = ring.tile([P, P], U8, align_bytes=64)
             nc.vector.quantize_mx(w_codes[:].bitcast(FP8X4), w_bytes[:], w_bf[:, t].rearrange("p m j -> p (m j)"))
             y = keep.tile([P, S], F32, name=f"y{t}")
             for u, cols in enumerate(halves if t == 0 else [whole]):

from contextlib import ExitStack

import concourse.mybir as mybir

K, T, S, H, W, G = 512, 1024, 256, 512, 128, 2048
FLOPS = 3 * 2 * K * H * S

F32 = mybir.dt.float32
BF16 = mybir.dt.bfloat16
I32 = mybir.dt.int32
U32 = mybir.dt.uint32
U16 = mybir.dt.uint16
U8 = mybir.dt.uint8
FP8X4 = mybir.dt.float8_e4m3fn_x4
ALU = mybir.AluOpType
COPY = mybir.ActivationFunctionType.Copy

P = 128
PACK = 4
TILES = H // P
GATHER_WINDOW = 272
SCATTER_WINDOW = 352
CAST_SPLIT = 40
HALF = S // 2


def tile_picked_cmixhaarsendhop_none_p_kernel(
    tc, x_words, x_scales, w1, gs, d_words, d_scales, offs, n1, n2, k1, k2, two, n3, n4, out
):
    nc = tc.nc
    with ExitStack() as ctx:
        keep = ctx.enter_context(tc.tile_pool(name="keep", bufs=1))
        ring = ctx.enter_context(tc.tile_pool(name="ring", bufs=2))
        psum = ctx.enter_context(tc.psum_pool(name="psum", bufs=1))

        def load_list(name, src):
            entries = keep.tile(list(src.shape), U16, name=name)
            nc.sync.dma_start(entries[:], src)
            return entries

        x_byte_table = keep.tile([P, T], U8, align_bytes=64)
        nc.vector.memset(x_byte_table[:].bitcast(I32), 0)
        w_rows = w1.rearrange("(p j) c -> p j c", j=PACK)
        w_raw = [keep.tile([P, PACK, H // 2], F32, name=f"w_raw{u}") for u in range(2)]
        nc.sync.dma_start(w_raw[0][:], w_rows[:, :, 0 : H // 2])
        offs_sb = load_list("offs_sb", offs)
        for q in range(4):
            nc.sync.dma_start(x_byte_table[32 * q : 32 * q + 4, :].bitcast(I32), x_scales[0][4 * q : 4 * q + 4, :].bitcast(I32))
        nc.sync.dma_start(w_raw[1][:], w_rows[:, :, H // 2 : H])
        x_word_table = keep.tile([P, T], I32, align_bytes=64)
        nc.sync.dma_start(x_word_table[:], x_words[0].rearrange("p n r -> p (n r)").bitcast(I32))

        n1_sb = load_list("n1_sb", n1)
        n2_sb = load_list("n2_sb", n2)
        k1_sb = load_list("k1_sb", k1)
        k2_sb = load_list("k2_sb", k2)
        d_byte_table = keep.tile([P, G], U8, align_bytes=64)
        nc.gpsimd.memset(d_byte_table[:].bitcast(I32), 0)
        nc.sync.dma_start(d_byte_table[0:P:8, :].bitcast(I32), d_scales[0].bitcast(I32))
        two_sb = load_list("two_sb", two)
        d_word_table = keep.tile([P, G], I32, align_bytes=64)
        nc.sync.dma_start(d_word_table[:], d_words[0].rearrange("p n r -> p (n r)").bitcast(I32))
        gs_sb = keep.tile([P, PACK], F32)
        nc.sync.dma_start(gs_sb[:], gs.rearrange("(p t) o -> p (t o)", t=PACK))
        n3_sb = load_list("n3_sb", n3)
        n4_sb = load_list("n4_sb", n4)

        xq_bytes = keep.tile([P, S], U8, align_bytes=64)
        nc.vector.tensor_copy(xq_bytes[:], x_byte_table[:].indirect(offs_sb[:]))

        w_bf = keep.tile([P, TILES, P, PACK], BF16, align_bytes=64)
        w_cols = [raw[:].rearrange("p j (m t) -> p m j t", t=TILES) for raw in w_raw]
        w_dealt = w_bf[:].rearrange("p t m j -> p m j t")
        for u in range(2):
            nc.vector.tensor_copy(w_dealt[:, 64 * u : 64 * u + CAST_SPLIT], w_cols[u][:, 0:CAST_SPLIT])
            nc.scalar.copy(w_dealt[:, 64 * u + CAST_SPLIT : 64 * (u + 1)], w_cols[u][:, CAST_SPLIT:64])
        halves = [slice(u * HALF, (u + 1) * HALF) for u in range(2)]
        whole = slice(0, S)
        xq_words = keep.tile([P, S], U32, align_bytes=64)
        for u in range(2):
            nc.vector.tensor_copy(xq_words[:, halves[u]], x_word_table[:].bitcast(U32).indirect(offs_sb[:, 8 * u : 8 * (u + 1)]))

        y_sb = []
        for t in range(TILES):
            w_codes = ring.tile([P, P], U32, align_bytes=64)
            w_bytes = ring.tile([P, P], U8, align_bytes=64)
            nc.vector.quantize_mx(w_codes[:].bitcast(FP8X4), w_bytes[:], w_bf[:, t].rearrange("p m j -> p (m j)"))
            y = keep.tile([P, S], F32, name=f"y{t}")
            for u, cols in enumerate(halves if t == 0 else [whole]):
                acc = psum.tile([P, cols.stop - cols.start], F32, name=f"y_acc{t}_{u}")
                nc.tensor.matmul_mx(acc[:], w_codes[:].bitcast(FP8X4), w_bytes[:], xq_words[:, cols].bitcast(FP8X4), xq_bytes[:, cols], start=True, stop=True)
                (nc.scalar.copy if t == 0 else nc.vector.tensor_copy)(y[:, cols], acc[:])
            y_sb.append(y)
        ra, rb = [], []
        for t in range(TILES):
            a = keep.tile([P, W], F32, name=f"pa{t}", tag=f"slot_a{t}", align_bytes=64)
            b = keep.tile([P, W], F32, name=f"pb{t}", tag=f"slot_b{t}", align_bytes=64)
            nc.scalar.activation(a[:], y_sb[t][:].indirect(n1_sb[:]), COPY)
            nc.scalar.activation(b[:], y_sb[t][:].indirect(n2_sb[:]), COPY)
            s = keep.tile([P, W], F32, name=f"sum{t}")
            d = keep.tile([P, W], F32, name=f"rb{t}")
            nc.vector.tensor_tensor(s[:], a[:], b[:], ALU.add)
            nc.vector.tensor_tensor(d[:], a[:], b[:], ALU.subtract)
            ra.append(s)
            rb.append(d)

        d_picked_bytes = keep.tile([P, 2 * H], U8, tag="slot_a1", align_bytes=64)
        d_bytes = keep.tile([P, 2 * H], U8, align_bytes=64)
        nc.vector.tensor_copy(d_picked_bytes[:, 0:H], d_byte_table[:].indirect(k1_sb[:]))
        nc.vector.tensor_copy(d_picked_bytes[:, H : 2 * H], d_byte_table[:].indirect(k2_sb[:]))
        for r in range(4):
            nc.sync.dma_start(d_bytes[r:P:32, :].bitcast(I32), d_picked_bytes[8 * r : P : 32, :].bitcast(I32))
        x2_bytes = keep.tile([P, S], U8, tag="slot_a2", align_bytes=64)
        x2_words = keep.tile([P, S], U32, tag="slot_b2", align_bytes=64)
        nc.vector.tensor_copy(x2_bytes[:], x_byte_table[:].indirect(two_sb[:]))
        nc.vector.tensor_copy(x2_words[:], x_word_table[:].bitcast(U32).indirect(two_sb[:]))

        def gather_d_words(u, tag):
            words = keep.tile([P, H], U32, name=f"d_picked_words{u}", tag=tag, align_bytes=64)
            nc.vector.tensor_copy(words[:, H // 2 : H], d_word_table[:].bitcast(U32).indirect(k2_sb[:, 16 * u : 16 * (u + 1)]))
            nc.vector.tensor_copy(words[:, 0 : H // 2], d_word_table[:].bitcast(U32).indirect(k1_sb[:, 16 * u : 16 * (u + 1)]))
            return words

        h_first = [psum.tile([P, HALF], F32, name=f"h_first{u}") for u in range(2)]
        h_acc = {t: psum.tile([P, S], F32, name=f"h_acc{t}", tag=tag) for t, tag in ((1, "h_acc1"), (2, "y_acc0_0"), (3, "y_acc0_1"))}

        def add_pass(acc, words, word_col, byte_col, codes, scales, cols, first):
            nc.tensor.matmul_mx(
                acc[:],
                words[:, word_col : word_col + P].bitcast(FP8X4),
                d_bytes[:, byte_col : byte_col + P],
                codes[:, cols].bitcast(FP8X4),
                scales[:, cols],
                start=first,
                stop=not first,
            )

        early_words = gather_d_words(0, "slot_a3")
        for u in range(2):
            add_pass(h_first[u], early_words, H // 2, H, x2_words, x2_bytes, halves[u], True)
        add_pass(h_acc[1], early_words, H // 2 + P, H + P, x2_words, x2_bytes, whole, True)

        z_bf = keep.tile([P, S, PACK], BF16, tag="slot_z", align_bytes=64)
        dt = [keep.tile([P, S], F32, name=f"dt{t}") for t in range(TILES)]
        for pair in ((0, 1), (2, 3)):
            for t in pair:
                nc.scalar.activation(dt[t][:].indirect(n1_sb[:]), ra[t][:], COPY, scale=0.75)
            for t in pair:
                nc.scalar.activation(dt[t][:].indirect(n2_sb[:]), rb[t][:], COPY)
                for cols in halves if t == TILES - 1 else [whole]:
                    nc.vector.tensor_scalar(z_bf[:, cols, t], dt[t][:, cols], gs_sb[:, t : t + 1], None, ALU.mult)

        z_codes = keep.tile([P, S], U32, align_bytes=64)
        z_bytes = keep.tile([P, S], U8, align_bytes=64)
        h_sb = [keep.tile([P, GATHER_WINDOW], F32, name=f"h{t}") for t in range(TILES)]
        for u in range(2):
            nc.vector.quantize_mx(z_codes[:, halves[u]].bitcast(FP8X4), z_bytes[:, halves[u]], z_bf[:, halves[u], :].rearrange("p s j -> p (s j)"))
        for u in range(2):
            add_pass(h_first[u], early_words, 0, 0, z_codes, z_bytes, halves[u], False)
            nc.scalar.activation(h_sb[0][:, halves[u]], h_first[u][:], COPY, scale=0.0625)
        add_pass(h_acc[1], early_words, P, P, z_codes, z_bytes, whole, False)
        nc.vector.tensor_scalar(h_sb[1][:, 0:S], h_acc[1][:], 0.0625, None, ALU.mult)
        late_words = gather_d_words(1, "slot_z")
        for t in range(2, TILES):
            c = (t % 2) * P
            add_pass(h_acc[t], late_words, H // 2 + c, H + t * P, x2_words, x2_bytes, whole, True)
            add_pass(h_acc[t], late_words, c, t * P, z_codes, z_bytes, whole, False)
            nc.vector.tensor_scalar(h_sb[t][:, 0:S], h_acc[t][:], 0.0625, None, ALU.mult)
        st_sb = []
        for t in range(TILES):
            hop = keep.tile([P, S], F32, name=f"hop{t}")
            nc.scalar.activation(hop[:], h_sb[t][:].indirect(n3_sb[:]), COPY)
            st = keep.tile([P, S], F32, name=f"st{t}")
            nc.vector.tensor_tensor(st[:], h_sb[t][:, 0:S], hop[:], ALU.max)
            st_sb.append(st)
        for t in range(TILES):
            ds2 = keep.tile([P, SCATTER_WINDOW], F32, name=f"ds2_{t}")
            nc.scalar.activation(ds2[:].indirect(n4_sb[:]), st_sb[t][:], COPY)
            res = keep.tile([P, S], F32, name=f"res{t}")
            nc.vector.tensor_tensor(res[:], ds2[:, 0:S], h_sb[t][:, 0:S], ALU.subtract)
            nc.sync.dma_start(out[t * P : (t + 1) * P, :], res[:])
